import numpy as np
import ml_dtypes


def mxq(x, axis, fmt="e4m3"):
    dtype, down = {"e4m3": (ml_dtypes.float8_e4m3fn, 7), "e5m2": (ml_dtypes.float8_e5m2, 14)}[fmt]
    v = np.moveaxis(np.asarray(x, np.float32).astype(ml_dtypes.bfloat16).astype(np.float64), axis, -1)
    blocks = v.reshape(v.shape[:-1] + (-1, 32))
    amax = np.abs(blocks).max(-1, keepdims=True)
    byte = np.maximum(np.where(amax > 0, np.frexp(amax)[1] - 1 + 127, 0) - down, 1)
    scale = np.exp2(byte - 127.0)
    codes = (blocks / scale).astype(np.float32).astype(dtype).astype(np.float64)
    return np.moveaxis((codes * scale).reshape(v.shape), -1, axis)


WIDE = False


def mx_kscale(k):
    if not WIDE:
        return np.ones(k)
    levels = np.array([10, -10, 5, -5, 0])
    if k % 512:
        return np.exp2(np.random.permutation(np.resize(levels, k // 32))).repeat(32)
    a = np.empty((k // 512, 16))
    for p in range(k // 512):
        a[p, :8] = np.random.permutation(np.resize(levels, 8))
        for g in range(8):
            far = levels[np.abs(levels - a[p, g]) >= 10]
            a[p, g + 8] = far[np.random.randint(len(far))]
    return np.exp2(a.ravel()).repeat(32)


def f64(x):
    return np.asarray(x).astype(np.float64)


def striped(idx):
    return np.tile(idx.reshape(-1, 16).T, (8, 1)).astype(np.uint16)


def unstriped(offs):
    return offs[:16].T.reshape(-1).astype(np.int64)


def striped8(idx):
    return np.concatenate([x.reshape(-1, 16).T for x in idx]).astype(np.uint16)


def runs(offs, k):
    lists = np.stack([offs[16 * r : 16 * r + 16].T.reshape(-1) for r in range(8)]).astype(np.int64)
    return lists[np.arange(k) % 512 // 64]


def pack_weight(w):
    k, n = w.shape
    w = f64(np.asarray(w, np.float32).astype(ml_dtypes.bfloat16)).reshape(k // 32, 32, n)
    amax = np.abs(w).max(1)
    byte = np.clip(np.where(amax > 0, np.frexp(amax)[1] - 1 + 127 - 7, 1), 1, 254)
    scaled = (w * np.exp2(127.0 - byte)[:, None, :]).reshape(k, n).astype(np.float32)
    words = np.ascontiguousarray(scaled.reshape(k // 512, 128, 4, n).transpose(0, 1, 3, 2)).astype(ml_dtypes.float8_e4m3fn).view(np.uint8)
    return words, np.ascontiguousarray(byte.astype(np.uint8).reshape(k // 512, 16, n))


def unpack_weight(words, scales):
    g, p, n, _ = words.shape
    vals = np.ascontiguousarray(words).view(ml_dtypes.float8_e4m3fn).astype(np.float64) * np.repeat(np.exp2(scales.astype(np.float64) - 127.0), 8, axis=1)[..., None]
    return vals.transpose(0, 1, 3, 2).reshape(g * 512, n)


def relu(v):
    return np.maximum(v, 0.0)


K, T, S, N, G, H, W = 512, 2048, 512, 512, 2048, 512, 256


def setup_inputs():
    n = np.random.standard_normal
    s = mx_kscale(K)[:, None]
    u = mx_kscale(S)
    packed_xT = pack_weight(n((K, T)) * s)
    packed_dT = pack_weight(n((K, G)) / s)
    perm = np.stack([np.random.permutation(S) for _ in range(8)])
    return {
        "x_words": packed_xT[0],
        "x_scales": packed_xT[1],
        "d_words": packed_dT[0],
        "d_scales": packed_dT[1],
        "gn": (np.random.uniform(0.5, 1.5, (H, 1)) * u[:, None]).astype(np.float32),
        "w1": (n((H, N)) / np.sqrt(H) / u[:, None]).astype(np.float32),
        "offs": striped(np.random.permutation(T)[:S]),
        "kidx": striped8(np.random.randint(0, G, (8, H))),
        "n1": striped8(perm[:, :W]),
        "n2": striped8(perm[:, W:]),
        "n3": striped8(np.stack([np.random.permutation(S) for _ in range(8)])),
    }


def reference(x_words, x_scales, d_words, d_scales, gn, w1, offs, kidx, n1, n2, n3):
    d_kidx = unpack_weight(d_words, d_scales)[np.arange(K)[:, None], runs(kidx, K)]
    xq = unpack_weight(x_words, x_scales)[:, unstriped(offs)]
    s = 0.0625 * (d_kidx.T @ xq)
    pa = s[np.arange(H)[:, None], runs(n1, H)]
    pb = s[np.arange(H)[:, None], runs(n2, H)]
    rb = np.maximum(pa, pb)
    ra = pa / (np.abs(pb) + 0.5)
    ds = np.zeros((H, S))
    ds[np.arange(H)[:, None], runs(n1, H)] = ra
    dt = ds.copy()
    dt[np.arange(H)[:, None], runs(n2, H)] = rb
    z = f64(gn) * dt
    h = mxq(f64(w1), 0, "e4m3").T @ mxq(z, 0, "e4m3")
    rl = relu(h)
    ds2 = np.zeros((N, S))
    ds2[np.arange(N)[:, None], runs(n3, N)] = rl
    return ds2 - (0.5 * h)

@@ -1,0 +1,227 @@
+from contextlib import ExitStack
+
+import concourse.mybir as mybir
+
+F32 = mybir.dt.float32
+BF16 = mybir.dt.bfloat16
+I32 = mybir.dt.int32
+U32 = mybir.dt.uint32
+U16 = mybir.dt.uint16
+U8 = mybir.dt.uint8
+FP8X4 = mybir.dt.float8_e4m3fn_x4
+ACT = mybir.ActivationFunctionType
+ALU = mybir.AluOpType
+
+P = 128
+PACK = 4
+TABLE = 2048
+S = 512
+W = 256
+WIDE = 1024
+CHUNKS = ((0, 128), (128, 256), (256, 512))
+FLOPS = 2 * 2 * 512 * 512 * 512
+
+
+def tile_picked_keyratiosend_none_p_kernel(
+    tc, x_words, x_scales, d_words, d_scales, gn, w1, offs, kidx, n1, n2, n3, out
+):
+    nc = tc.nc
+    with ExitStack() as ctx:
+        keep = ctx.enter_context(tc.tile_pool(name="keep", bufs=1))
+        psum = ctx.enter_context(tc.psum_pool(name="psum", bufs=1))
+
+        def load_list(src, name):
+            t = keep.tile(list(src.shape), U16, name=name)
+            nc.sync.dma_start(t[:], src)
+            return t
+
+        def cleared_rows(name, clear):
+            t = keep.tile([P, TABLE], U8, name=name, align_bytes=64)
+            clear.memset(t[:].bitcast(I32), 0)
+            return t
+
+        def load_words(src, name):
+            t = keep.tile([P, TABLE], I32, name=name)
+            nc.sync.dma_start(t[:], src[0].rearrange("p n t -> p (n t)").bitcast(I32))
+            return t
+
+        d_rows = cleared_rows("d_rows", nc.gpsimd)
+        x_rows = cleared_rows("x_rows", nc.vector)
+        kidx_sb = load_list(kidx, "kidx_sb")
+        offs_sb = load_list(offs, "offs_sb")
+        n2_sb = load_list(n2, "n2_sb")
+        n1_sb = load_list(n1, "n1_sb")
+        n3_sb = load_list(n3, "n3_sb")
+        for rows, src in ((d_rows, d_scales), (x_rows, x_scales)):
+            nc.sync.dma_start(rows[:].bitcast(I32)[0:P:8, :], src[0].bitcast(I32))
+        d_table = load_words(d_words, "d_table")
+        x_table = load_words(x_words, "x_table")
+
+        warm = keep.tile([P, 2], F32)
+        nc.gpsimd.memset(warm[:, 0:1], 1.0)
+        nc.scalar.activation(warm[:, 1:2], warm[:, 0:1], ACT.Abs_reciprocal_sqrt, bias=0.5)
+
+        d_bytes = keep.tile([P, S], U8)
+        x_bytes = keep.tile([P, S], U8)
+        nc.vector.tensor_copy(d_bytes[:], d_rows[:].indirect(kidx_sb[:]))
+        nc.vector.tensor_copy(x_bytes[:], x_rows[:].indirect(offs_sb[:]))
+        planes = keep.tile([P, 2 * S], U8, align_bytes=64)
+        nc.vector.tensor_copy(
+            planes[:, 0:S].rearrange("p (t c) -> p c t", t=PACK), d_bytes[:].rearrange("p (c t) -> p c t", t=PACK)
+        )
+        nc.vector.tensor_copy(planes[:, S : 2 * S].bitcast(I32), x_bytes[:].bitcast(I32))
+        plane_words = planes[:].bitcast(I32)
+        for a in range(1, 4):
+            nc.sync.dma_start(plane_words[a:P:32, :], plane_words[8 * a : P : 32, :])
+
+        gn_sb = keep.tile([P, PACK], F32, tag="d_bytes")
+        nc.scalar.dma_start(gn_sb[:], gn.rearrange("(p t) o -> p (t o)", t=PACK))
+
+        d_picked = keep.tile([P, S], U32, tag="x_rows", align_bytes=64)
+        nc.vector.tensor_copy(d_picked[:], d_table[:].bitcast(U32).indirect(kidx_sb[:]))
+        d_dealt = keep.tile([P, S], U32, align_bytes=64)
+        nc.vector.tensor_copy(
+            d_dealt[:].rearrange("p (t c) -> p c t", t=PACK), d_picked[:].rearrange("p (c t) -> p c t", t=PACK)
+        )
+        x_picked = keep.tile([P, S], U32, align_bytes=64)
+        for half in range(2):
+            nc.vector.tensor_copy(
+                x_picked[:, half * W : (half + 1) * W],
+                x_table[:].bitcast(U32).indirect(offs_sb[:, half * 16 : (half + 1) * 16]),
+            )
+        w_raw = keep.tile([P, PACK, S], F32, tag="x_table")
+        nc.sync.dma_start(w_raw[:], w1.rearrange("(p t) m -> p t m", t=PACK))
+
+        s = [keep.tile([P, S], F32, name="s%d" % t) for t in range(PACK)]
+        pa = [keep.tile([P, 2, W], F32, name="pa%d" % g) for g in range(2)]
+        pb = [keep.tile([P, 2, W], F32, name="pb%d" % g) for g in range(2)]
+        size = [keep.tile([P, W], F32, name="size%d" % t) for t in range(PACK)]
+        root = [keep.tile([P, W], F32, name="root%d" % t) for t in range(PACK)]
+        inv = [keep.tile([P, W], F32, name="inv%d" % t, align_bytes=64) for t in range(PACK)]
+        z = [keep.tile([P, b - a, PACK], BF16, name="z%d" % a, align_bytes=64) for a, b in CHUNKS]
+        w_grouped = keep.tile([P, PACK, P, PACK], BF16, align_bytes=64)
+        z_codes = keep.tile([P, S], U32, align_bytes=64)
+        z_plane = keep.tile([P, S], U8, align_bytes=64)
+
+        def scores(t, a, b, bank):
+            acc = psum.tile([P, b - a], F32, name="acc", tag="bank%d" % bank)
+            nc.tensor.matmul_mx(
+                out=acc[:],
+                lhsT=d_dealt[:, t * P : (t + 1) * P].bitcast(FP8X4),
+                lhsT_scale=planes[:, t * P : (t + 1) * P],
+                rhs=x_picked[:, a:b].bitcast(FP8X4),
+                rhs_scale=planes[:, S + a : S + b],
+                start=True,
+                stop=True,
+            )
+            nc.scalar.activation(s[t][:, a:b], acc[:], ACT.Copy, scale=0.0625)
+
+        def fetch(t):
+            nc.vector.tensor_copy(pb[t // 2][:, t % 2, :], s[t][:].indirect(n2_sb[:]))
+            nc.vector.tensor_copy(pa[t // 2][:, t % 2, :], s[t][:].indirect(n1_sb[:]))
+
+        def inverse(t):
+            nc.scalar.activation(size[t][:], pb[t // 2][:, t % 2, :], ACT.Abs)
+            nc.scalar.activation(root[t][:], size[t][:], ACT.Abs_reciprocal_sqrt, bias=0.5)
+            nc.scalar.activation(inv[t][:], root[t][:], ACT.Square)
+
+        def group_w(q):
+            c = slice(32 * q, 32 * (q + 1))
+            nc.scalar.copy(
+                w_grouped[:].rearrange("p u c t -> p c t u")[:, c],
+                w_raw[:].rearrange("p t (c u) -> p c t u", u=PACK)[:, c],
+            )
+
+        scores(0, 0, W, 0)
+        scores(0, W, S, 7)
+        for t in range(1, PACK):
+            scores(t, 0, S, t)
+        for t in range(PACK):
+            fetch(t)
+        for t in range(PACK):
+            inverse(t)
+        for q in range(PACK):
+            group_w(q)
+        rb = [keep.tile([P, 2, W], F32, name="rb%d" % g, tag="size%d" % g) for g in range(2)]
+        for g in range(2):
+            nc.vector.tensor_tensor(rb[g][:], pa[g][:], pb[g][:], ALU.max)
+        dt = [keep.tile([P, S], F32, name="dt%d" % t) for t in range(PACK - 1)]
+        dt.append(keep.tile([P, S], F32, name="dt3", tag="root1"))
+
+        def put_larger(t):
+            nc.vector.tensor_copy(dt[t][:].indirect(n2_sb[:]), rb[t // 2][:, t % 2, :])
+
+        def put_ratio(t):
+            nc.vector.tensor_tensor(dt[t][:].indirect(n1_sb[:]), pa[t // 2][:, t % 2, :], inv[t][:], ALU.mult)
+
+        put_larger(0)
+        for t in range(1, PACK):
+            put_larger(t)
+            put_ratio(t - 1)
+        put_ratio(PACK - 1)
+        for t in range(PACK):
+            for (a, b), zc in zip(CHUNKS, z):
+                nc.scalar.activation(zc[:, :, t], dt[t][:, a:b], ACT.Copy, scale=gn_sb[:, t : t + 1])
+
+        w_flat = w_grouped[:].rearrange("p u c t -> p (u c t)")
+        w_codes = [keep.tile([P, P], U32, name="w_codes0", align_bytes=64)]
+        w_plane = keep.tile([P, S], U8, align_bytes=64)
+        nc.vector.quantize_mx(out=w_codes[0][:].bitcast(FP8X4), scales=w_plane[:, 0:P], in_=w_flat[:, 0:S])
+
+        rl = [keep.tile([P, S], F32, name="rl%d" % u) for u in range(PACK)]
+        hm = [keep.tile([P, S], F32, name="hm%d" % u) for u in range(PACK)]
+        ds2 = [keep.tile([P, WIDE], F32, name="ds2_%d" % u) for u in range(PACK)]
+        res = [keep.tile([P, S], F32, name="res%d" % u) for u in range(PACK)]
+        out_rows = out.rearrange("(p u) j -> u p j", u=PACK)
+
+        def values(u, a, b, bank):
+            acc = psum.tile([P, b - a], F32, name="acc", tag="bank%d" % bank)
+            nc.tensor.matmul_mx(
+                out=acc[:],
+                lhsT=w_codes[u][:].bitcast(FP8X4),
+                lhsT_scale=w_plane[:, u * P : (u + 1) * P],
+                rhs=z_codes[:, a:b].bitcast(FP8X4),
+                rhs_scale=z_plane[:, a:b],
+                start=True,
+                stop=True,
+            )
+            nc.scalar.activation(rl[u][:, a:b], acc[:], ACT.Relu)
+            return acc
+
+        def send(u, a, b):
+            nc.vector.tensor_copy(ds2[u][:].indirect(n3_sb[:, a // 16 : b // 16]), rl[u][:, a:b])
+
+        def halve(u, a, b, acc):
+            nc.scalar.activation(hm[u][:, a:b], acc[:], ACT.Copy, scale=-0.5)
+
+        def finish(u, a, b, queue):
+            nc.vector.tensor_tensor(res[u][:, a:b], ds2[u][:, a:b], hm[u][:, a:b], ALU.add)
+            queue.dma_start(out_rows[u][:, a:b], res[u][:, a:b])
+
+        first = []
+        for n, ((a, b), zc) in enumerate(zip(CHUNKS, z)):
+            nc.vector.quantize_mx(
+                out=z_codes[:, a:b].bitcast(FP8X4), scales=z_plane[:, a:b], in_=zc[:].rearrange("p c t -> p (c t)")
+            )
+            first.append(values(0, a, b, 4 + n))
+        w_rest = keep.tile([P, 3 * P], U32, tag="inv3", align_bytes=64)
+        nc.vector.quantize_mx(out=w_rest[:, 0:P].bitcast(FP8X4), scales=w_plane[:, P : 2 * P], in_=w_flat[:, S : 2 * S])
+        nc.vector.quantize_mx(
+            out=w_rest[:, P : 3 * P].bitcast(FP8X4), scales=w_plane[:, 2 * P : 4 * P], in_=w_flat[:, 2 * S : 4 * S]
+        )
+        w_codes.extend(w_rest[:, v * P : (v + 1) * P] for v in range(3))
+        send(0, 0, P)
+        send(0, P, S)
+        accs = [values(1, 0, S, 1)]
+        send(1, 0, S)
+        for (a, b), acc in zip(CHUNKS, first):
+            halve(0, a, b, acc)
+        finish(0, 0, S, nc.sync)
+        for u in range(2, PACK):
+            accs.append(values(u, 0, S, u))
+            send(u, 0, S)
+            halve(u - 1, 0, S, accs[u - 2])
+            finish(u - 1, 0, S, nc.sync)
+        halve(PACK - 1, 0, S, accs[PACK - 2])
+        finish(PACK - 1, 0, W, nc.sync)
+        finish(PACK - 1, W, S, nc.scalar)

@@ -41,56 +41,62 @@ def tile_picked_keyratiosend_none_p_kernel(
             return t
 
         def load_words(src, name):
-            t = keep.tile([P, TABLE], I32, name=name)
+            t = keep.tile([P, TABLE], I32, name=name, align_bytes=64)
             nc.sync.dma_start(t[:], src[0].rearrange("p n t -> p (n t)").bitcast(I32))
             return t
 
         d_rows = cleared_rows("d_rows", nc.gpsimd)
         x_rows = cleared_rows("x_rows", nc.vector)
+        planes = keep.tile([P, 2 * S], U8, align_bytes=64)
+        nc.gpsimd.memset(planes[:].bitcast(I32), 0)
         kidx_sb = load_list(kidx, "kidx_sb")
         offs_sb = load_list(offs, "offs_sb")
         n2_sb = load_list(n2, "n2_sb")
         n1_sb = load_list(n1, "n1_sb")
-        n3_sb = load_list(n3, "n3_sb")
         for rows, src in ((d_rows, d_scales), (x_rows, x_scales)):
             nc.sync.dma_start(rows[:].bitcast(I32)[0:P:8, :], src[0].bitcast(I32))
         d_table = load_words(d_words, "d_table")
         x_table = load_words(x_words, "x_table")
+        n3_sb = load_list(n3, "n3_sb")
 
         warm = keep.tile([P, 2], F32)
         nc.gpsimd.memset(warm[:, 0:1], 1.0)
         nc.scalar.activation(warm[:, 1:2], warm[:, 0:1], ACT.Abs_reciprocal_sqrt, bias=0.5)
 
-        d_bytes = keep.tile([P, S], U8)
-        x_bytes = keep.tile([P, S], U8)
+        d_bytes = keep.tile([P, S], U8, align_bytes=64)
+        x_bytes = keep.tile([P, S], U8, align_bytes=64)
         nc.vector.tensor_copy(d_bytes[:], d_rows[:].indirect(kidx_sb[:]))
         nc.vector.tensor_copy(x_bytes[:], x_rows[:].indirect(offs_sb[:]))
-        planes = keep.tile([P, 2 * S], U8, align_bytes=64)
+        staged = keep.tile([P, 2 * S // 4], I32, align_bytes=64)
         nc.vector.tensor_copy(
-            planes[:, 0:S].rearrange("p (t c) -> p c t", t=PACK), d_bytes[:].rearrange("p (c t) -> p c t", t=PACK)
+            staged[:, 0:P].rearrange("p (t b h) -> p t b h", t=PACK, h=2),
+            d_bytes[:].bitcast(I32).rearrange("p (b t h) -> p t b h", t=PACK, h=2),
         )
-        nc.vector.tensor_copy(planes[:, S : 2 * S].bitcast(I32), x_bytes[:].bitcast(I32))
-        plane_words = planes[:].bitcast(I32)
-        for a in range(1, 4):
-            nc.sync.dma_start(plane_words[a:P:32, :], plane_words[8 * a : P : 32, :])
+        nc.vector.tensor_copy(staged[:, P : 2 * P], x_bytes[:].bitcast(I32))
+        for a in range(4):
+            queue = (nc.sync, nc.scalar)[a % 2]
+            queue.dma_start(planes[:].bitcast(I32)[a:P:32, :], staged[8 * a : P : 32, :])
 
-        gn_sb = keep.tile([P, PACK], F32, tag="d_bytes")
-        nc.scalar.dma_start(gn_sb[:], gn.rearrange("(p t) o -> p (t o)", t=PACK))
 
         d_picked = keep.tile([P, S], U32, tag="x_rows", align_bytes=64)
         nc.vector.tensor_copy(d_picked[:], d_table[:].bitcast(U32).indirect(kidx_sb[:]))
-        d_dealt = keep.tile([P, S], U32, align_bytes=64)
-        nc.vector.tensor_copy(
-            d_dealt[:].rearrange("p (t c) -> p c t", t=PACK), d_picked[:].rearrange("p (c t) -> p c t", t=PACK)
-        )
+        d_by_tile = d_picked[:].rearrange("p (b t q) -> p t b q", t=PACK, q=8)
+        d_first = keep.tile([P, P], U32, align_bytes=64)
+        nc.vector.tensor_copy(d_first[:].rearrange("p (b q) -> p b q", q=8), d_by_tile[:, 0])
         x_picked = keep.tile([P, S], U32, align_bytes=64)
         for half in range(2):
             nc.vector.tensor_copy(
                 x_picked[:, half * W : (half + 1) * W],
                 x_table[:].bitcast(U32).indirect(offs_sb[:, half * 16 : (half + 1) * 16]),
             )
-        w_raw = keep.tile([P, PACK, S], F32, tag="x_table")
-        nc.sync.dma_start(w_raw[:], w1.rearrange("(p t) m -> p t m", t=PACK))
+        d_rest = keep.tile([P, 3 * P], U32, tag="x_table", align_bytes=64)
+        nc.vector.tensor_copy(d_rest[:].rearrange("p (t b q) -> p t b q", t=3, q=8), d_by_tile[:, 1:PACK])
+        d_dealt = [d_first[:]] + [d_rest[:, v * P : (v + 1) * P] for v in range(3)]
+        w_raw = keep.tile([P, PACK, S], F32, tag="d_table", align_bytes=64)
+        w_rows = w1.rearrange("(b t q) m -> t b q m", t=PACK, q=8)
+        for t in range(PACK):
+            nc.sync.dma_start(w_raw[:, t, :], w_rows[t])
+
 
         s = [keep.tile([P, S], F32, name="s%d" % t) for t in range(PACK)]
         pa = [keep.tile([P, 2, W], F32, name="pa%d" % g) for g in range(2)]
@@ -107,7 +113,7 @@ def tile_picked_keyratiosend_none_p_kernel(
             acc = psum.tile([P, b - a], F32, name="acc", tag="bank%d" % bank)
             nc.tensor.matmul_mx(
                 out=acc[:],
-                lhsT=d_dealt[:, t * P : (t + 1) * P].bitcast(FP8X4),
+                lhsT=d_dealt[t].bitcast(FP8X4),
                 lhsT_scale=planes[:, t * P : (t + 1) * P],
                 rhs=x_picked[:, a:b].bitcast(FP8X4),
                 rhs_scale=planes[:, S + a : S + b],
@@ -136,6 +142,12 @@ def tile_picked_keyratiosend_none_p_kernel(
         scores(0, W, S, 7)
         for t in range(1, PACK):
             scores(t, 0, S, t)
+        gn_rows = gn.rearrange("(b t q) o -> t b q o", t=PACK, q=8)
+        gn_sb = []
+        for t, slot in enumerate(("staged", "x_rows", "d_first", "x_picked")):
+            gn_sb.append(keep.tile([P, 1], F32, name="gn%d" % t, tag=slot, align_bytes=64))
+            with nc.allow_non_contiguous_dma(reason="one weight for each key row"):
+                nc.sync.dma_start(gn_sb[t][:], gn_rows[t])
         for t in range(PACK):
             fetch(t)
         for t in range(PACK):
@@ -161,32 +173,41 @@ def tile_picked_keyratiosend_none_p_kernel(
         put_ratio(PACK - 1)
         for t in range(PACK):
             for (a, b), zc in zip(CHUNKS, z):
-                nc.scalar.activation(zc[:, :, t], dt[t][:, a:b], ACT.Copy, scale=gn_sb[:, t : t + 1])
+                nc.scalar.activation(zc[:, :, t], dt[t][:, a:b], ACT.Copy, scale=gn_sb[t][:])
 
         w_flat = w_grouped[:].rearrange("p u c t -> p (u c t)")
-        w_codes = [keep.tile([P, P], U32, name="w_codes0", align_bytes=64)]
+        w_early = keep.tile([P, 2 * P], U32, align_bytes=64)
         w_plane = keep.tile([P, S], U8, align_bytes=64)
-        nc.vector.quantize_mx(out=w_codes[0][:].bitcast(FP8X4), scales=w_plane[:, 0:P], in_=w_flat[:, 0:S])
+        nc.vector.quantize_mx(out=w_early[:].bitcast(FP8X4), scales=w_plane[:, 0 : 2 * P], in_=w_flat[:, 0 : 2 * S])
 
         rl = [keep.tile([P, S], F32, name="rl%d" % u) for u in range(PACK)]
         hm = [keep.tile([P, S], F32, name="hm%d" % u) for u in range(PACK)]
         ds2 = [keep.tile([P, WIDE], F32, name="ds2_%d" % u) for u in range(PACK)]
         res = [keep.tile([P, S], F32, name="res%d" % u) for u in range(PACK)]
         out_rows = out.rearrange("(p u) j -> u p j", u=PACK)
+        w_codes = [w_early[:, 0:P], w_early[:, P : 2 * P]]
 
-        def values(u, a, b, bank):
-            acc = psum.tile([P, b - a], F32, name="acc", tag="bank%d" % bank)
-            nc.tensor.matmul_mx(
-                out=acc[:],
-                lhsT=w_codes[u][:].bitcast(FP8X4),
-                lhsT_scale=w_plane[:, u * P : (u + 1) * P],
-                rhs=z_codes[:, a:b].bitcast(FP8X4),
-                rhs_scale=z_plane[:, a:b],
-                start=True,
-                stop=True,
+        def quantize_z(n):
+            a, b = CHUNKS[n]
+            nc.vector.quantize_mx(
+                out=z_codes[:, a:b].bitcast(FP8X4), scales=z_plane[:, a:b], in_=z[n][:].rearrange("p c t -> p (c t)")
             )
-            nc.scalar.activation(rl[u][:, a:b], acc[:], ACT.Relu)
-            return acc
+
+        def values(u, pieces, bank):
+            first, last = pieces[0][0], pieces[-1][1]
+            acc = psum.tile([P, last - first], F32, name="acc", tag="bank%d" % bank)
+            for a, b in pieces:
+                nc.tensor.matmul_mx(
+                    out=acc[:, a - first : b - first],
+                    lhsT=w_codes[u].bitcast(FP8X4),
+                    lhsT_scale=w_plane[:, u * P : (u + 1) * P],
+                    rhs=z_codes[:, a:b].bitcast(FP8X4),
+                    rhs_scale=z_plane[:, a:b],
+                    start=True,
+                    stop=True,
+                )
+            nc.scalar.activation(rl[u][:, first:last], acc[:], ACT.Relu)
+            return u, first, last, acc
 
         def send(u, a, b):
             nc.vector.tensor_copy(ds2[u][:].indirect(n3_sb[:, a // 16 : b // 16]), rl[u][:, a:b])
@@ -194,34 +215,30 @@ def tile_picked_keyratiosend_none_p_kernel(
         def halve(u, a, b, acc):
             nc.scalar.activation(hm[u][:, a:b], acc[:], ACT.Copy, scale=-0.5)
 
-        def finish(u, a, b, queue):
-            nc.vector.tensor_tensor(res[u][:, a:b], ds2[u][:, a:b], hm[u][:, a:b], ALU.add)
+        def finish(engine, u, a, b, queue):
+            engine.tensor_tensor(res[u][:, a:b], ds2[u][:, a:b], hm[u][:, a:b], ALU.add)
             queue.dma_start(out_rows[u][:, a:b], res[u][:, a:b])
 
-        first = []
-        for n, ((a, b), zc) in enumerate(zip(CHUNKS, z)):
-            nc.vector.quantize_mx(
-                out=z_codes[:, a:b].bitcast(FP8X4), scales=z_plane[:, a:b], in_=zc[:].rearrange("p c t -> p (c t)")
-            )
-            first.append(values(0, a, b, 4 + n))
-        w_rest = keep.tile([P, 3 * P], U32, tag="inv3", align_bytes=64)
-        nc.vector.quantize_mx(out=w_rest[:, 0:P].bitcast(FP8X4), scales=w_plane[:, P : 2 * P], in_=w_flat[:, S : 2 * S])
+        quantize_z(0)
+        held = [values(u, CHUNKS[:1], 4 + u) for u in range(2)]
+        quantize_z(1)
+        w_late = keep.tile([P, 2 * P], U32, tag="z0", align_bytes=64)
         nc.vector.quantize_mx(
-            out=w_rest[:, P : 3 * P].bitcast(FP8X4), scales=w_plane[:, 2 * P : 4 * P], in_=w_flat[:, 2 * S : 4 * S]
+            out=w_late[:].bitcast(FP8X4), scales=w_plane[:, 2 * P : 4 * P], in_=w_flat[:, 2 * S : 4 * S]
         )
-        w_codes.extend(w_rest[:, v * P : (v + 1) * P] for v in range(3))
-        send(0, 0, P)
-        send(0, P, S)
-        accs = [values(1, 0, S, 1)]
-        send(1, 0, S)
-        for (a, b), acc in zip(CHUNKS, first):
-            halve(0, a, b, acc)
-        finish(0, 0, S, nc.sync)
+        w_codes.extend([w_late[:, 0:P], w_late[:, P : 2 * P]])
+        quantize_z(2)
+        for u in range(2):
+            send(u, 0, P)
+        held.extend(values(u, CHUNKS[1:], 6 + u) for u in range(2))
+        for u in range(2):
+            send(u, P, S)
         for u in range(2, PACK):
-            accs.append(values(u, 0, S, u))
+            held.append(values(u, ((0, S),), u))
             send(u, 0, S)
-            halve(u - 1, 0, S, accs[u - 2])
-            finish(u - 1, 0, S, nc.sync)
-        halve(PACK - 1, 0, S, accs[PACK - 2])
-        finish(PACK - 1, 0, W, nc.sync)
-        finish(PACK - 1, W, S, nc.scalar)
+        for piece in sorted(held, key=lambda piece: piece[:2]):
+            halve(*piece)
+        for u in range(PACK - 1):
+            finish(nc.gpsimd, u, 0, S, nc.sync)
+        finish(nc.vector, PACK - 1, 0, W, nc.sync)
+        finish(nc.vector, PACK - 1, W, S, nc.scalar)

@@ -1,6 +1,7 @@
 from contextlib import ExitStack
 
 import concourse.mybir as mybir
+from concourse.masks import make_identity
 
 F32 = mybir.dt.float32
 BF16 = mybir.dt.bfloat16
@@ -62,6 +63,9 @@ def tile_picked_keyratiosend_none_p_kernel(
         warm = keep.tile([P, 2], F32)
         nc.gpsimd.memset(warm[:, 0:1], 1.0)
         nc.scalar.activation(warm[:, 1:2], warm[:, 0:1], ACT.Abs_reciprocal_sqrt, bias=0.5)
+
+        identity = keep.tile([P, P], F32)
+        make_identity(nc, identity[:])
 
         d_bytes = keep.tile([P, S], U8, align_bytes=64)
         x_bytes = keep.tile([P, S], U8, align_bytes=64)
@@ -176,16 +180,16 @@ def tile_picked_keyratiosend_none_p_kernel(
                 nc.scalar.activation(zc[:, :, t], dt[t][:, a:b], ACT.Copy, scale=gn_sb[t][:])
 
         w_flat = w_grouped[:].rearrange("p u c t -> p (u c t)")
-        w_early = keep.tile([P, 2 * P], U32, align_bytes=64)
+        w_all = keep.tile([P, S], U32, tag="inv3", align_bytes=64)
         w_plane = keep.tile([P, S], U8, align_bytes=64)
-        nc.vector.quantize_mx(out=w_early[:].bitcast(FP8X4), scales=w_plane[:, 0 : 2 * P], in_=w_flat[:, 0 : 2 * S])
+        nc.vector.quantize_mx(out=w_all[:].bitcast(FP8X4), scales=w_plane[:], in_=w_flat)
 
         rl = [keep.tile([P, S], F32, name="rl%d" % u) for u in range(PACK)]
         hm = [keep.tile([P, S], F32, name="hm%d" % u) for u in range(PACK)]
         ds2 = [keep.tile([P, WIDE], F32, name="ds2_%d" % u) for u in range(PACK)]
         res = [keep.tile([P, S], F32, name="res%d" % u) for u in range(PACK)]
         out_rows = out.rearrange("(p u) j -> u p j", u=PACK)
-        w_codes = [w_early[:, 0:P], w_early[:, P : 2 * P]]
+        w_codes = [w_all[:, u * P : (u + 1) * P] for u in range(PACK)]
 
         def quantize_z(n):
             a, b = CHUNKS[n]
@@ -222,11 +226,6 @@ def tile_picked_keyratiosend_none_p_kernel(
         quantize_z(0)
         held = [values(u, CHUNKS[:1], 4 + u) for u in range(2)]
         quantize_z(1)
-        w_late = keep.tile([P, 2 * P], U32, tag="z0", align_bytes=64)
-        nc.vector.quantize_mx(
-            out=w_late[:].bitcast(FP8X4), scales=w_plane[:, 2 * P : 4 * P], in_=w_flat[:, 2 * S : 4 * S]
-        )
-        w_codes.extend([w_late[:, 0:P], w_late[:, P : 2 * P]])
         quantize_z(2)
         for u in range(2):
             send(u, 0, P)
@@ -239,6 +238,23 @@ def tile_picked_keyratiosend_none_p_kernel(
         for piece in sorted(held, key=lambda piece: piece[:2]):
             halve(*piece)
         for u in range(PACK - 1):
-            finish(nc.gpsimd, u, 0, S, nc.sync)
+            banks = ((0, 1), (4, 5)) if u % 2 == 0 else ((4, 5), (0, 1))
+            turned_sb = []
+            for half in range(2):
+                turned = psum.tile([P, W], F32, tag="bank%d" % banks[0][half])
+                for c in range(0, W, P):
+                    cols = slice(half * W + c, half * W + c + P)
+                    for first, term in ((True, hm[u]), (False, ds2[u])):
+                        nc.tensor.matmul(
+                            turned[:, c : c + P], term[:, cols], identity[:], start=first, stop=not first, is_transpose=True
+                        )
+                turned_sb.append(keep.tile([P, W], F32, name="turned_sb%d_%d" % (u, half)))
+                nc.scalar.copy(turned_sb[half][:], turned[:])
+            for half in range(2):
+                back = psum.tile([P, W], F32, tag="bank%d" % banks[1][half])
+                for c in range(0, W, P):
+                    nc.tensor.transpose(back[:, c : c + P], turned_sb[half][:, c : c + P], identity[:])
+                nc.scalar.copy(res[u][:, half * W : (half + 1) * W], back[:])
+            nc.scalar.dma_start(out_rows[u], res[u][:])
         finish(nc.vector, PACK - 1, 0, W, nc.sync)
-        finish(nc.vector, PACK - 1, W, S, nc.scalar)
+        finish(nc.vector, PACK - 1, W, S, nc.sync)

@@ -49,7 +49,6 @@ def tile_picked_keyratiosend_none_p_kernel(
         d_rows = cleared_rows("d_rows", nc.gpsimd)
         x_rows = cleared_rows("x_rows", nc.vector)
         planes = keep.tile([P, 2 * S], U8, align_bytes=64)
-        nc.gpsimd.memset(planes[:].bitcast(I32), 0)
         kidx_sb = load_list(kidx, "kidx_sb")
         offs_sb = load_list(offs, "offs_sb")
         n2_sb = load_list(n2, "n2_sb")
@@ -60,9 +59,6 @@ def tile_picked_keyratiosend_none_p_kernel(
         x_table = load_words(x_words, "x_table")
         n3_sb = load_list(n3, "n3_sb")
 
-        warm = keep.tile([P, 2], F32)
-        nc.gpsimd.memset(warm[:, 0:1], 1.0)
-        nc.scalar.activation(warm[:, 1:2], warm[:, 0:1], ACT.Abs_reciprocal_sqrt, bias=0.5)
 
         identity = keep.tile([P, P], F32)
         make_identity(nc, identity[:])
@@ -71,15 +67,15 @@ def tile_picked_keyratiosend_none_p_kernel(
         x_bytes = keep.tile([P, S], U8, align_bytes=64)
         nc.vector.tensor_copy(d_bytes[:], d_rows[:].indirect(kidx_sb[:]))
         nc.vector.tensor_copy(x_bytes[:], x_rows[:].indirect(offs_sb[:]))
-        staged = keep.tile([P, 2 * S // 4], I32, align_bytes=64)
+        plane_words = planes[:].bitcast(I32)
         nc.vector.tensor_copy(
-            staged[:, 0:P].rearrange("p (t b h) -> p t b h", t=PACK, h=2),
+            plane_words[:, 0:P].rearrange("p (t b h) -> p t b h", t=PACK, h=2),
             d_bytes[:].bitcast(I32).rearrange("p (b t h) -> p t b h", t=PACK, h=2),
         )
-        nc.vector.tensor_copy(staged[:, P : 2 * P], x_bytes[:].bitcast(I32))
-        for a in range(4):
+        nc.vector.tensor_copy(plane_words[:, P : 2 * P], x_bytes[:].bitcast(I32))
+        for a in range(1, 4):
             queue = (nc.sync, nc.scalar)[a % 2]
-            queue.dma_start(planes[:].bitcast(I32)[a:P:32, :], staged[8 * a : P : 32, :])
+            queue.dma_start(plane_words[a:P:32, :], plane_words[8 * a : P : 32, :])
 
 
         d_picked = keep.tile([P, S], U32, tag="x_rows", align_bytes=64)
@@ -148,7 +144,7 @@ def tile_picked_keyratiosend_none_p_kernel(
             scores(t, 0, S, t)
         gn_rows = gn.rearrange("(b t q) o -> t b q o", t=PACK, q=8)
         gn_sb = []
-        for t, slot in enumerate(("staged", "x_rows", "d_first", "x_picked")):
+        for t, slot in enumerate(("planes", "x_rows", "d_first", "x_picked")):
             gn_sb.append(keep.tile([P, 1], F32, name="gn%d" % t, tag=slot, align_bytes=64))
             with nc.allow_non_contiguous_dma(reason="one weight for each key row"):
                 nc.sync.dma_start(gn_sb[t][:], gn_rows[t])

from contextlib import ExitStack

import concourse.mybir as mybir
from concourse.masks import make_identity

F32 = mybir.dt.float32
BF16 = mybir.dt.bfloat16
I32 = mybir.dt.int32
U32 = mybir.dt.uint32
U16 = mybir.dt.uint16
U8 = mybir.dt.uint8
FP8X4 = mybir.dt.float8_e4m3fn_x4
ACT = mybir.ActivationFunctionType
ALU = mybir.AluOpType

P = 128
PACK = 4
TABLE = 2048
S = 512
W = 256
WIDE = 1024
CHUNKS = ((0, 128), (128, 256), (256, 512))
FLOPS = 2 * 2 * 512 * 512 * 512


def tile_picked_keyratiosend_none_p_kernel(
    tc, x_words, x_scales, d_words, d_scales, gn, w1, offs, kidx, n1, n2, n3, out
):
    nc = tc.nc
    with ExitStack() as ctx:
        keep = ctx.enter_context(tc.tile_pool(name="keep", bufs=1))
        psum = ctx.enter_context(tc.psum_pool(name="psum", bufs=1))

        def load_list(src, name):
            t = keep.tile(list(src.shape), U16, name=name)
            nc.sync.dma_start(t[:], src)
            return t

        def cleared_rows(name, clear):
            t = keep.tile([P, TABLE], U8, name=name, align_bytes=64)
            clear.memset(t[:].bitcast(I32), 0)
            return t

        def load_words(src, name):
            t = keep.tile([P, TABLE], I32, name=name, align_bytes=64)
            nc.sync.dma_start(t[:], src[0].rearrange("p n t -> p (n t)").bitcast(I32))
            return t

        d_rows = cleared_rows("d_rows", nc.gpsimd)
        x_rows = cleared_rows("x_rows", nc.vector)
        planes = keep.tile([P, 2 * S], U8, align_bytes=64)
        kidx_sb = load_list(kidx, "kidx_sb")
        offs_sb = load_list(offs, "offs_sb")
        n2_sb = load_list(n2, "n2_sb")
        n1_sb = load_list(n1, "n1_sb")
        for rows, src in ((d_rows, d_scales), (x_rows, x_scales)):
            nc.sync.dma_start(rows[:].bitcast(I32)[0:P:8, :], src[0].bitcast(I32))
        d_table = load_words(d_words, "d_table")
        x_table = load_words(x_words, "x_table")
        n3_sb = load_list(n3, "n3_sb")


        identity = keep.tile([P, P], F32)
        make_identity(nc, identity[:])

        d_bytes = keep.tile([P, S], U8, align_bytes=64)
        x_bytes = keep.tile([P, S], U8, align_bytes=64)
        nc.vector.tensor_copy(d_bytes[:], d_rows[:].indirect(kidx_sb[:]))
        nc.vector.tensor_copy(x_bytes[:], x_rows[:].indirect(offs_sb[:]))
        plane_words = planes[:].bitcast(I32)
        nc.vector.tensor_copy(
            plane_words[:, 0:P].rearrange("p (t b h) -> p t b h", t=PACK, h=2),
            d_bytes[:].bitcast(I32).rearrange("p (b t h) -> p t b h", t=PACK, h=2),
        )
        nc.vector.tensor_copy(plane_words[:, P : 2 * P], x_bytes[:].bitcast(I32))
        for a in range(1, 4):
            queue = (nc.sync, nc.scalar)[a % 2]
            queue.dma_start(plane_words[a:P:32, :], plane_words[8 * a : P : 32, :])


        d_picked = keep.tile([P, S], U32, tag="x_rows", align_bytes=64)
        nc.vector.tensor_copy(d_picked[:], d_table[:].bitcast(U32).indirect(kidx_sb[:]))
        d_by_tile = d_picked[:].rearrange("p (b t q) -> p t b q", t=PACK, q=8)
        d_first = keep.tile([P, P], U32, align_bytes=64)
        nc.vector.tensor_copy(d_first[:].rearrange("p (b q) -> p b q", q=8), d_by_tile[:, 0])
        x_picked = keep.tile([P, S], U32, align_bytes=64)
        for half in range(2):
            nc.vector.tensor_copy(
                x_picked[:, half * W : (half + 1) * W],
                x_table[:].bitcast(U32).indirect(offs_sb[:, half * 16 : (half + 1) * 16]),
            )
        d_rest = keep.tile([P, 3 * P], U32, tag="x_table", align_bytes=64)
        nc.vector.tensor_copy(d_rest[:].rearrange("p (t b q) -> p t b q", t=3, q=8), d_by_tile[:, 1:PACK])
        d_dealt = [d_first[:]] + [d_rest[:, v * P : (v + 1) * P] for v in range(3)]
        w_raw = keep.tile([P, PACK, S], F32, tag="d_table", align_bytes=64)
        w_rows = w1.rearrange("(b t q) m -> t b q m", t=PACK, q=8)
        for t in range(PACK):
            nc.sync.dma_start(w_raw[:, t, :], w_rows[t])


        s = [keep.tile([P, S], F32, name="s%d" % t) for t in range(PACK)]
        pa = [keep.tile([P, 2, W], F32, name="pa%d" % g) for g in range(2)]
        pb = [keep.tile([P, 2, W], F32, name="pb%d" % g) for g in range(2)]
        size = [keep.tile([P, W], F32, name="size%d" % t) for t in range(PACK)]
        root = [keep.tile([P, W], F32, name="root%d" % t) for t in range(PACK)]
        inv = [keep.tile([P, W], F32, name="inv%d" % t, align_bytes=64) for t in range(PACK)]
        z = [keep.tile([P, b - a, PACK], BF16, name="z%d" % a, align_bytes=64) for a, b in CHUNKS]
        w_grouped = keep.tile([P, PACK, P, PACK], BF16, align_bytes=64)
        z_codes = keep.tile([P, S], U32, align_bytes=64)
        z_plane = keep.tile([P, S], U8, align_bytes=64)

        def scores(t, a, b, bank):
            acc = psum.tile([P, b - a], F32, name="acc", tag="bank%d" % bank)
            nc.tensor.matmul_mx(
                out=acc[:],
                lhsT=d_dealt[t].bitcast(FP8X4),
                lhsT_scale=planes[:, t * P : (t + 1) * P],
                rhs=x_picked[:, a:b].bitcast(FP8X4),
                rhs_scale=planes[:, S + a : S + b],
                start=True,
                stop=True,
            )
            nc.scalar.activation(s[t][:, a:b], acc[:], ACT.Copy, scale=0.0625)

        def fetch(t):
            nc.vector.tensor_copy(pb[t // 2][:, t % 2, :], s[t][:].indirect(n2_sb[:]))
            nc.vector.tensor_copy(pa[t // 2][:, t % 2, :], s[t][:].indirect(n1_sb[:]))

        def inverse(t):
            nc.scalar.activation(size[t][:], pb[t // 2][:, t % 2, :], ACT.Abs)
            nc.scalar.activation(root[t][:], size[t][:], ACT.Abs_reciprocal_sqrt, bias=0.5)
            nc.scalar.activation(inv[t][:], root[t][:], ACT.Square)

        def group_w(q):
            c = slice(32 * q, 32 * (q + 1))
            nc.scalar.copy(
                w_grouped[:].rearrange("p u c t -> p c t u")[:, c],
                w_raw[:].rearrange("p t (c u) -> p c t u", u=PACK)[:, c],
            )

        scores(0, 0, W, 0)
        scores(0, W, S, 7)
        for t in range(1, PACK):
            scores(t, 0, S, t)
        gn_rows = gn.rearrange("(b t q) o -> t b q o", t=PACK, q=8)
        gn_sb = []
        for t, slot in enumerate(("planes", "x_rows", "d_first", "x_picked")):
            gn_sb.append(keep.tile([P, 1], F32, name="gn%d" % t, tag=slot, align_bytes=64))
            with nc.allow_non_contiguous_dma(reason="one weight for each key row"):
                nc.sync.dma_start(gn_sb[t][:], gn_rows[t])
        for t in range(PACK):
            fetch(t)
        for t in range(PACK):
            inverse(t)
        for q in range(PACK):
            group_w(q)
        rb = [keep.tile([P, 2, W], F32, name="rb%d" % g, tag="size%d" % g) for g in range(2)]
        for g in range(2):
            nc.vector.tensor_tensor(rb[g][:], pa[g][:], pb[g][:], ALU.max)
        dt = [keep.tile([P, S], F32, name="dt%d" % t) for t in range(PACK - 1)]
        dt.append(keep.tile([P, S], F32, name="dt3", tag="root1"))

        def put_larger(t):
            nc.vector.tensor_copy(dt[t][:].indirect(n2_sb[:]), rb[t // 2][:, t % 2, :])

        def put_ratio(t):
            nc.vector.tensor_tensor(dt[t][:].indirect(n1_sb[:]), pa[t // 2][:, t % 2, :], inv[t][:], ALU.mult)

        put_larger(0)
        for t in range(1, PACK):
            put_larger(t)
            put_ratio(t - 1)
        put_ratio(PACK - 1)
        for t in range(PACK):
            for (a, b), zc in zip(CHUNKS, z):
                nc.scalar.activation(zc[:, :, t], dt[t][:, a:b], ACT.Copy, scale=gn_sb[t][:])

        w_flat = w_grouped[:].rearrange("p u c t -> p (u c t)")
        w_all = keep.tile([P, S], U32, tag="inv3", align_bytes=64)
        w_plane = keep.tile([P, S], U8, align_bytes=64)
        nc.vector.quantize_mx(out=w_all[:].bitcast(FP8X4), scales=w_plane[:], in_=w_flat)

        rl = [keep.tile([P, S], F32, name="rl%d" % u) for u in range(PACK)]
        hm = [keep.tile([P, S], F32, name="hm%d" % u) for u in range(PACK)]
        ds2 = [keep.tile([P, WIDE], F32, name="ds2_%d" % u) for u in range(PACK)]
        res = [keep.tile([P, S], F32, name="res%d" % u) for u in range(PACK)]
        out_rows = out.rearrange("(p u) j -> u p j", u=PACK)
        w_codes = [w_all[:, u * P : (u + 1) * P] for u in range(PACK)]

        def quantize_z(n):
            a, b = CHUNKS[n]
            nc.vector.quantize_mx(
                out=z_codes[:, a:b].bitcast(FP8X4), scales=z_plane[:, a:b], in_=z[n][:].rearrange("p c t -> p (c t)")
            )

        def values(u, pieces, bank):
            first, last = pieces[0][0], pieces[-1][1]
            acc = psum.tile([P, last - first], F32, name="acc", tag="bank%d" % bank)
            for a, b in pieces:
                nc.tensor.matmul_mx(
                    out=acc[:, a - first : b - first],
                    lhsT=w_codes[u].bitcast(FP8X4),
                    lhsT_scale=w_plane[:, u * P : (u + 1) * P],
                    rhs=z_codes[:, a:b].bitcast(FP8X4),
                    rhs_scale=z_plane[:, a:b],
                    start=True,
                    stop=True,
                )
            nc.scalar.activation(rl[u][:, first:last], acc[:], ACT.Relu)
            return u, first, last, acc

        def send(u, a, b):
            nc.vector.tensor_copy(ds2[u][:].indirect(n3_sb[:, a // 16 : b // 16]), rl[u][:, a:b])

        def halve(u, a, b, acc):
            nc.scalar.activation(hm[u][:, a:b], acc[:], ACT.Copy, scale=-0.5)

        def finish(engine, u, a, b, queue):
            engine.tensor_tensor(res[u][:, a:b], ds2[u][:, a:b], hm[u][:, a:b], ALU.add)
            queue.dma_start(out_rows[u][:, a:b], res[u][:, a:b])

        quantize_z(0)
        held = [values(u, CHUNKS[:1], 4 + u) for u in range(2)]
        quantize_z(1)
        quantize_z(2)
        for u in range(2):
            send(u, 0, P)
        held.extend(values(u, CHUNKS[1:], 6 + u) for u in range(2))
        for u in range(2):
            send(u, P, S)
        for u in range(2, PACK):
            held.append(values(u, ((0, S),), u))
            send(u, 0, S)
        for piece in sorted(held, key=lambda piece: piece[:2]):
            halve(*piece)
        for u in range(PACK - 1):
            banks = ((0, 1), (4, 5)) if u % 2 == 0 else ((4, 5), (0, 1))
            turned_sb = []
            for half in range(2):
                turned = psum.tile([P, W], F32, tag="bank%d" % banks[0][half])
                for c in range(0, W, P):
                    cols = slice(half * W + c, half * W + c + P)
                    for first, term in ((True, hm[u]), (False, ds2[u])):
                        nc.tensor.matmul(
                            turned[:, c : c + P], term[:, cols], identity[:], start=first, stop=not first, is_transpose=True
                        )
                turned_sb.append(keep.tile([P, W], F32, name="turned_sb%d_%d" % (u, half)))
                nc.scalar.copy(turned_sb[half][:], turned[:])
            for half in range(2):
                back = psum.tile([P, W], F32, tag="bank%d" % banks[1][half])
                for c in range(0, W, P):
                    nc.tensor.transpose(back[:, c : c + P], turned_sb[half][:, c : c + P], identity[:])
                nc.scalar.copy(res[u][:, half * W : (half + 1) * W], back[:])
            nc.scalar.dma_start(out_rows[u], res[u][:])
        finish(nc.vector, PACK - 1, 0, W, nc.sync)
        finish(nc.vector, PACK - 1, W, S, nc.sync)
